import numpy as np
import ml_dtypes


def mxq(x, axis, fmt="e4m3"):
    dtype, down = {"e4m3": (ml_dtypes.float8_e4m3fn, 7), "e5m2": (ml_dtypes.float8_e5m2, 14)}[fmt]
    v = np.moveaxis(np.asarray(x, np.float32).astype(ml_dtypes.bfloat16).astype(np.float64), axis, -1)
    blocks = v.reshape(v.shape[:-1] + (-1, 32))
    amax = np.abs(blocks).max(-1, keepdims=True)
    byte = np.maximum(np.where(amax > 0, np.frexp(amax)[1] - 1 + 127, 0) - down, 1)
    scale = np.exp2(byte - 127.0)
    codes = (blocks / scale).astype(np.float32).astype(dtype).astype(np.float64)
    return np.moveaxis((codes * scale).reshape(v.shape), -1, axis)


WIDE = False


def mx_kscale(k):
    if not WIDE:
        return np.ones(k)
    levels = np.array([10, -10, 5, -5, 0])
    if k % 512:
        return np.exp2(np.random.permutation(np.resize(levels, k // 32))).repeat(32)
    a = np.empty((k // 512, 16))
    for p in range(k // 512):
        a[p, :8] = np.random.permutation(np.resize(levels, 8))
        for g in range(8):
            far = levels[np.abs(levels - a[p, g]) >= 10]
            a[p, g + 8] = far[np.random.randint(len(far))]
    return np.exp2(a.ravel()).repeat(32)


BF16 = ml_dtypes.bfloat16


def bf(x):
    return np.asarray(x, np.float32).astype(BF16)


def f64(x):
    return np.asarray(x).astype(np.float64)

def planes(Y):
    n, m = Y.shape
    b = f64(bf(Y)).reshape(n // 32, 32, m)
    amax = np.abs(b).max(1)
    byte = np.clip(np.where(amax > 0, np.frexp(amax)[1] - 1 + 127 - 7, 1), 1, 254)
    codes = (b * np.exp2(127.0 - byte)[:, None, :]).reshape(n, m).astype(np.float32).astype(ml_dtypes.float8_e4m3fn).view(np.uint8)
    words = codes.reshape(n // 512, 128, 4, m).transpose(0, 1, 3, 2)
    return np.ascontiguousarray(words), np.ascontiguousarray(byte.astype(np.uint8).reshape(n // 512, 16, m))


W, Q, H, T, U = 4, 512, 1024, 512, 512
V = W - 1


def softmax(v):
    x = np.exp(v - np.max(v, axis=-1, keepdims=True))
    return x / np.sum(x, axis=-1, keepdims=True)


def forward_step(e_w, p_prev, rho_w, n_hap):
    prior = (1.0 - rho_w) * p_prev + rho_w / n_hap
    b = np.exp(e_w - np.max(e_w, axis=-1, keepdims=True)) * prior
    return b / np.sum(b, axis=-1, keepdims=True)


def setup_inputs():
    s, t = mx_kscale(T), mx_kscale(H)
    return {
        "obs": bf(np.random.standard_normal((W, Q, T)) * s),
        "typed": bf(0.7 * np.random.standard_normal((W, H, T)) / np.sqrt(T) / s),
        "rho": bf(np.random.uniform(0.2, 0.5, (V,))),
        "g": bf((1.0 + 0.1 * np.random.standard_normal((H,))) * t),
        "alt": bf(np.random.standard_normal((W, H, U)) / np.sqrt(H) / t[:, None]),
        "base": bf(0.3 * np.random.standard_normal((W, U))),
    }


def core(obs, typed, rho, g, alt, base):
    obs, typed, rho, g, alt, base = f64(obs), f64(typed), f64(rho), f64(g), f64(alt), f64(base)
    n_win = obs.shape[0]
    n_hap = typed.shape[1]
    e = mxq(obs, 2, "e4m3") @ mxq(typed, 2, "e4m3").transpose(0, 2, 1)
    posts = [softmax(e[0])]
    for w in range(1, n_win):
        posts.append(forward_step(e[w], posts[w - 1], rho[w - 1], n_hap))
    p = np.stack(posts, axis=0)
    z = g[None, None, :] * (n_hap * p - 1.0)
    return (mxq(z, 2, "e4m3") @ mxq(alt, 1, "e4m3")) + base[:, None, :]


def reference(obs, typed, rho, g, alt, base):
    R_out = core(obs, typed, rho, g, alt, base)
    words, scales = planes(np.moveaxis(R_out, 1, 0).reshape(512, -1))
    return R_out, words, scales

@@ -1,0 +1,336 @@
+from contextlib import ExitStack
+
+import concourse.mybir as mybir
+from concourse.masks import make_identity
+
+W, Q, H, T, U = 4, 512, 1024, 512, 512
+FLOPS = 2 * W * Q * H * T + 2 * W * Q * H * U
+
+F32 = mybir.dt.float32
+BF16 = mybir.dt.bfloat16
+I32 = mybir.dt.int32
+U32 = mybir.dt.uint32
+U8 = mybir.dt.uint8
+FP8X4 = mybir.dt.float8_e4m3fn_x4
+ALU = mybir.AluOpType
+ACT = mybir.ActivationFunctionType
+
+P = 128
+PACK = 4
+BANK = 512
+GROUPS = H // BANK
+HALF = 256
+TILES = W * PACK
+TINY = 2.0 ** -40
+
+
+def tile_listephenswindowforwardimputation_x1_kernel(tc, obs, typed, rho, g, alt, base, out_0, out_1, out_2):
+    nc = tc.nc
+    with ExitStack() as ctx:
+        keep = ctx.enter_context(tc.tile_pool(name="keep", bufs=1))
+        work = ctx.enter_context(tc.tile_pool(name="work", bufs=2))
+        psum = ctx.enter_context(tc.psum_pool(name="psum", bufs=2))
+        ctx.enter_context(tc.manual_schedule())
+
+        ident = keep.tile([P, P], F32, name="ident")
+        make_identity(nc, ident[:])
+
+        rows_raw = {}
+        alt_raw = {}
+
+        def load_rows(w, part, j):
+            src = obs[w] if part == GROUPS else typed[w, part * BANK:(part + 1) * BANK, :]
+            raw = keep.tile([P, 2, T], BF16, name="rows_%d_%d_%d" % (w, part, j))
+            nc.sync.dma_start(out=raw[:], in_=src.rearrange("(m t) k -> m t k", t=PACK)[:, 2 * j:2 * j + 2, :])
+            rows_raw[(w, part, j)] = raw
+
+        def load_alt(w, grp):
+            raw = keep.tile([P, PACK, U], BF16, name="alt_%d_%d" % (w, grp))
+            nc.sync.dma_start(out=raw[:], in_=alt[w, grp * BANK:(grp + 1) * BANK, :].rearrange("(p j) u -> p j u", j=PACK))
+            alt_raw[(w, grp)] = raw
+
+        OBS = GROUPS
+        g_raw = keep.tile([P, GROUPS, PACK], BF16, name="g_raw")
+        rho_raw = keep.tile([P, W - 1], BF16, name="rho_raw")
+        base_bc = keep.tile([P, W, U], BF16, name="base_bc")
+        for w in range(W):
+            if w == 0:
+                order = [(OBS, 0), (0, 0), (0, 1), (1, 0), (1, 1), (OBS, 1)]
+            else:
+                order = [(0, 0), (0, 1), (1, 0), (1, 1), (OBS, 0), (OBS, 1)]
+            for part, j in order:
+                load_rows(w, part, j)
+            for grp in range(GROUPS):
+                load_alt(w, grp)
+            if w == 0:
+                nc.sync.dma_start(out=g_raw[:], in_=g.rearrange("(a p t) -> p a t", a=GROUPS, t=PACK))
+                nc.sync.dma_start(out=rho_raw[:], in_=rho.partition_broadcast(P))
+            if w == 1:
+                nc.sync.dma_start(out=base_bc[:].rearrange("p w u -> p (w u)"),
+                                  in_=base.rearrange("w u -> (w u)").partition_broadcast(P))
+
+        out_codes = keep.tile([P, W * U], U32, name="out_codes", align_bytes=64)
+        out_scales = keep.tile([P, W * U], U8, name="out_scales", align_bytes=64)
+        words_hbm = out_1[0].rearrange("p m t -> p (m t)").bitcast(I32)
+        scales_hbm = out_2[0].bitcast(I32)
+
+        g_scaled = keep.tile([P, GROUPS, PACK], F32, name="g_scaled")
+        shift = keep.tile([P, W - 1], F32, name="shift")
+
+        def constants():
+            nc.vector.tensor_scalar(out=g_scaled[:], in0=g_raw[:], scalar1=float(H), scalar2=None, op0=ALU.mult)
+            stay = keep.tile([P, W - 1], F32, name="stay")
+            nc.vector.tensor_scalar(out=stay[:], in0=rho_raw[:], scalar1=-1.0, scalar2=1.0, op0=ALU.mult, op1=ALU.add)
+            guard = keep.tile([P, W - 1], F32, name="guard")
+            nc.vector.tensor_scalar(out=guard[:], in0=stay[:], scalar1=0.0, scalar2=TINY, op0=ALU.is_equal, op1=ALU.mult)
+            safe = keep.tile([P, W - 1], F32, name="safe")
+            nc.vector.tensor_tensor(out=safe[:], in0=stay[:], in1=guard[:], op=ALU.add)
+            inv = keep.tile([P, W - 1], F32, name="inv")
+            nc.vector.reciprocal(out=inv[:], in_=safe[:])
+            nc.vector.scalar_tensor_tensor(out=shift[:], in0=rho_raw[:], scalar=1.0 / H, in1=inv[:], op0=ALU.mult, op1=ALU.mult)
+
+        codes = {}
+        scales = {}
+        banks = {}
+        staged = {}
+        out32 = {}
+
+        def planes(key, tag, bufs):
+            if key not in codes:
+                codes[key] = work.tile([P, BANK], U32, name="c_" + tag, tag="c_" + tag, bufs=bufs, align_bytes=64)
+                scales[key] = work.tile([P, BANK], U8, name="s_" + tag, tag="s_" + tag, bufs=bufs, align_bytes=64)
+            return codes[key], scales[key]
+
+        def turn(piece, tag):
+            kind, w, part, j = piece
+            if kind != "rows":
+                return
+            bank = psum.tile([P, PACK, P], F32, name="bank_" + tag, tag=tag)
+            words = rows_raw[(w, part, j)][:].bitcast(F32)
+            for s in range(2):
+                for u in range(2):
+                    nc.tensor.transpose(bank[:, 2 * s + u, :], words[:, s, u:T // 2:2], ident[:])
+            banks[piece] = bank
+
+        def stage(piece, on_vector):
+            kind, w, part, j = piece
+            copy = nc.vector.tensor_copy if on_vector else nc.scalar.copy
+            st = work.tile([P, PACK * HALF], BF16, name="staged", tag="staged", bufs=6, align_bytes=64)
+            if kind == "rows":
+                copy(out=st[:].bitcast(F32).rearrange("p (s m u) -> p s m u", s=2, u=2),
+                     in_=banks[piece][:].rearrange("p (s u) m -> p s m u", u=2))
+            else:
+                src = alt_raw[(w, part)] if kind == "alt" else out32[w]
+                copy(out=st[:].rearrange("p (u t) -> p u t", t=PACK),
+                     in_=src[:, :, j * HALF:(j + 1) * HALF].rearrange("p t u -> p u t"))
+            staged[piece] = st
+
+        def quantize(piece):
+            kind, w, part, j = piece
+            if kind == "out":
+                cols = slice(w * U + j * HALF, w * U + (j + 1) * HALF)
+                c, s = out_codes, out_scales
+            else:
+                cols = slice(j * HALF, (j + 1) * HALF)
+                if kind == "alt":
+                    c, s = planes((kind, w, part), "alt", 4)
+                elif part == OBS:
+                    c, s = planes((kind, w, part), "obs", 2)
+                else:
+                    c, s = planes((kind, w, part), "typed", 4)
+            nc.vector.quantize_mx(out=c[:, cols].bitcast(FP8X4), scales=s[:, cols], in_=staged[piece][:])
+            if kind == "out":
+                nc.sync.dma_start(out=words_hbm[:, cols], in_=out_codes[:, cols].bitcast(I32))
+
+        def store_scales(windows, queues):
+            cols = slice(windows.start * U // 4, windows.stop * U // 4)
+            for quad in range(4):
+                queues[quad % len(queues)].dma_start(out=scales_hbm[4 * quad:4 * quad + 4, cols],
+                                                     in_=out_scales[32 * quad:32 * quad + 4, :].bitcast(I32)[:, cols])
+
+        def pieces(step):
+            found = []
+            w, r = divmod(step + 2, PACK)
+            if 0 <= w < W:
+                found.append(("alt", w, r // 2, r % 2))
+            w, r = divmod(step - 6, PACK)
+            if 0 <= w < W - 1 and r < 2:
+                found.append(("out", w, 0, r))
+            w, r = divmod(step + 4, PACK)
+            if 1 <= w < W:
+                if r < GROUPS:
+                    found.extend([("rows", w, r, 0), ("rows", w, r, 1)])
+                else:
+                    found.append(("rows", w, OBS, r - GROUPS))
+            return found
+
+        e_bank = {}
+        neg_e = {}
+        neg_max = {}
+        weight = {}
+        total = {}
+        inv_total = {}
+        post = {}
+        z_bank = {}
+        z_bf = {}
+        z_codes = {}
+        z_scales = {}
+        o_bank = {}
+
+        def live(i):
+            return 0 <= i < TILES
+
+        def emissions(i):
+            w, t = divmod(i, PACK)
+            cols = slice(t * P, (t + 1) * P)
+            for grp in range(GROUPS):
+                bank = psum.tile([P, BANK], F32, name="e_bank", tag="e")
+                nc.tensor.matmul_mx(out=bank[:], lhsT=codes[("rows", w, OBS)][:, cols].bitcast(FP8X4),
+                                    lhsT_scale=scales[("rows", w, OBS)][:, cols],
+                                    rhs=codes[("rows", w, grp)][:].bitcast(FP8X4), rhs_scale=scales[("rows", w, grp)][:],
+                                    start=True, stop=True)
+                e_bank[(i, grp)] = bank
+
+        def row_max(i, grp):
+            if grp == 0:
+                neg_e[i] = work.tile([P, H], F32, name="neg_e", tag="neg_e")
+            m = work.tile([P, 1], F32, name="neg_max", tag="neg_max", bufs=4)
+            nc.vector.tensor_scalar(out=neg_e[i][:, grp * BANK:(grp + 1) * BANK], in0=e_bank[(i, grp)][:], scalar1=-1.0,
+                                    scalar2=neg_max[i][:] if grp else None, op0=ALU.mult, op1=ALU.min, accum_out=m[:])
+            neg_max[i] = m
+
+        def exponentiate(i):
+            x = work.tile([P, H], F32, name="x", tag="x")
+            if i < PACK:
+                total[i] = work.tile([P, 1], F32, name="total", tag="total")
+                nc.scalar.activation(out=x[:], in_=neg_e[i][:], func=ACT.Exp, bias=neg_max[i][:], scale=-1.0, accum_out=total[i][:])
+            else:
+                nc.scalar.activation(out=x[:], in_=neg_e[i][:], func=ACT.Exp, bias=neg_max[i][:], scale=-1.0)
+            weight[i] = x
+
+        def recombine(i):
+            w = i // PACK
+            b = work.tile([P, H], F32, name="b", tag="b")
+            total[i] = work.tile([P, 1], F32, name="total", tag="total")
+            nc.vector.scalar_tensor_tensor(out=b[:], in0=post[i - PACK][:], scalar=shift[:, w - 1:w], in1=weight[i][:],
+                                           op0=ALU.add, op1=ALU.mult, accum_out=total[i][:])
+            weight[i] = b
+
+        def invert(i):
+            inv_total[i] = work.tile([P, 1], F32, name="inv_total", tag="inv_total")
+            nc.vector.reciprocal(out=inv_total[i][:], in_=total[i][:])
+
+        def normalize(i):
+            post[i] = work.tile([P, H], F32, name="post", tag="post", bufs=5)
+            nc.scalar.activation(out=post[i][:], in_=weight[i][:], func=ACT.Copy, scale=inv_total[i][:])
+
+        def turn_posterior(i):
+            for grp in range(GROUPS):
+                bank = psum.tile([P, PACK, P], F32, name="z_bank", tag="z")
+                for t in range(PACK):
+                    c0 = grp * BANK + t * P
+                    nc.tensor.transpose(bank[:, t, :], post[i][:, c0:c0 + P], ident[:])
+                z_bank[(i, grp)] = bank
+
+        def gate(i, grp):
+            if grp == 0:
+                z_bf[i] = work.tile([P, H], BF16, name="z_bf", tag="z_bf", align_bytes=64)
+            nc.vector.scalar_tensor_tensor(
+                out=z_bf[i][:, grp * BANK:(grp + 1) * BANK].rearrange("p (q t) -> p q t", t=PACK),
+                in0=z_bank[(i, grp)][:].rearrange("p t q -> p q t"), scalar=1.0 / H,
+                in1=g_scaled[:, grp, :].unsqueeze(1).to_broadcast([P, P, PACK]), op0=ALU.subtract, op1=ALU.mult)
+
+        def quantize_z(i, parts):
+            z_codes[i] = work.tile([P, GROUPS * P], U32, name="z_codes", tag="z_codes", align_bytes=64)
+            z_scales[i] = work.tile([P, GROUPS * P], U8, name="z_scales", tag="z_scales", align_bytes=64)
+            width = GROUPS * P // parts
+            for n in range(parts):
+                cols = slice(n * width, (n + 1) * width)
+                nc.vector.quantize_mx(out=z_codes[i][:, cols].bitcast(FP8X4), scales=z_scales[i][:, cols],
+                                      in_=z_bf[i][:, PACK * n * width:PACK * (n + 1) * width])
+
+        def impute(i, sites, tag):
+            w = i // PACK
+            bank = psum.tile([P, sites.stop - sites.start], F32, name="o_bank", tag=tag)
+            for grp in range(GROUPS):
+                cols = slice(grp * P, (grp + 1) * P)
+                nc.tensor.matmul_mx(out=bank[:], lhsT=z_codes[i][:, cols].bitcast(FP8X4), lhsT_scale=z_scales[i][:, cols],
+                                    rhs=codes[("alt", w, grp)][:, sites].bitcast(FP8X4), rhs_scale=scales[("alt", w, grp)][:, sites],
+                                    start=(grp == 0), stop=(grp == GROUPS - 1))
+            o_bank[(i, sites.start)] = bank
+
+        def add_base(i, sites):
+            w, t = divmod(i, PACK)
+            if w not in out32:
+                out32[w] = work.tile([P, PACK, U], F32, name="out32", tag="out32")
+            nc.vector.tensor_tensor(out=out32[w][:, t, sites], in0=o_bank[(i, sites.start)][:], in1=base_bc[:, w, sites], op=ALU.add)
+            nc.sync.dma_start(out=out_0[w].rearrange("(p t) u -> p t u", t=PACK)[:, t, sites], in_=out32[w][:, t, sites])
+
+        head = [("rows", 0, OBS, 0), ("rows", 0, 0, 0), ("rows", 0, 0, 1), ("rows", 0, 1, 0), ("rows", 0, 1, 1)]
+        for piece, tag in zip(head, ["in", "in", "z", "z", "o"]):
+            turn(piece, tag)
+        for n, piece in enumerate(head):
+            stage(piece, on_vector=(n == 1))
+        for piece in head:
+            quantize(piece)
+        emissions(0)
+        late = ("rows", 0, OBS, 1)
+        turn(late, "o")
+        stage(late, on_vector=False)
+        for j in range(2):
+            stage(("alt", 0, 0, j), on_vector=False)
+        pending = [late, ("alt", 0, 0, 0), ("alt", 0, 0, 1)]
+        every_site = slice(0, U)
+
+        for s in range(TILES + 1):
+            now = pieces(s)
+            if live(s - 1) and s - 1 >= PACK:
+                recombine(s - 1)
+            if live(s):
+                row_max(s, 0)
+            if live(s - 1):
+                invert(s - 1)
+                normalize(s - 1)
+            if live(s - 2):
+                gate(s - 2, 0)
+            if live(s):
+                row_max(s, 1)
+                exponentiate(s)
+            if live(s - 2):
+                gate(s - 2, 1)
+            if s == 0:
+                constants()
+            for piece in pending:
+                quantize(piece)
+            if live(s - 3):
+                add_base(s - 3, every_site)
+            if live(s - 2):
+                quantize_z(s - 2, 1)
+            if live(s - 1):
+                turn_posterior(s - 1)
+            for piece in now:
+                turn(piece, "in")
+            if live(s + 1):
+                emissions(s + 1)
+            if live(s - 2):
+                impute(s - 2, every_site, "o")
+            for piece in now:
+                stage(piece, on_vector=False)
+            pending = now
+        store_scales(range(0, W - 1), [nc.sync])
+
+        last = TILES - 1
+        halves = [slice(0, HALF), slice(HALF, U)]
+        for grp in range(GROUPS):
+            gate(last, grp)
+        quantize_z(last, GROUPS)
+        add_base(last - 1, every_site)
+        for sites in halves:
+            impute(last, sites, "e")
+        for sites in halves:
+            add_base(last, sites)
+        for j in range(2):
+            stage(("out", W - 1, 0, j), on_vector=(j == 1))
+        for j in (1, 0):
+            quantize(("out", W - 1, 0, j))
+        store_scales(range(W - 1, W), [nc.sync, nc.scalar])

@@ -57,11 +57,13 @@ def tile_listephenswindowforwardimputation_x1_kernel(tc, obs, typed, rho, g, alt
             if w == 0:
                 order = [(OBS, 0), (0, 0), (0, 1), (1, 0), (1, 1), (OBS, 1)]
             else:
-                order = [(0, 0), (0, 1), (1, 0), (1, 1), (OBS, 0), (OBS, 1)]
+                order = [(0, 0), (0, 1), (1, 0), (1, 1), (OBS, 0), (OBS, 1)][1 if w == 1 else 0:]
             for part, j in order:
                 load_rows(w, part, j)
             for grp in range(GROUPS):
                 load_alt(w, grp)
+                if w == 0 and grp == 0:
+                    load_rows(1, 0, 0)
             if w == 0:
                 nc.sync.dma_start(out=g_raw[:], in_=g.rearrange("(a p t) -> p a t", a=GROUPS, t=PACK))
                 nc.sync.dma_start(out=rho_raw[:], in_=rho.partition_broadcast(P))
@@ -156,12 +158,10 @@ def tile_listephenswindowforwardimputation_x1_kernel(tc, obs, typed, rho, g, alt
             w, r = divmod(step - 6, PACK)
             if 0 <= w < W - 1 and r < 2:
                 found.append(("out", w, 0, r))
-            w, r = divmod(step + 4, PACK)
+            w, r = divmod(step + 5, PACK)
             if 1 <= w < W:
-                if r < GROUPS:
-                    found.extend([("rows", w, r, 0), ("rows", w, r, 1)])
-                else:
-                    found.append(("rows", w, OBS, r - GROUPS))
+                first, stop = [(0, 1), (1, 3), (3, 5), (5, 6)][r]
+                found.extend([("rows", w, n // 2, n % 2) for n in range(first, stop)])
             return found
 
         e_bank = {}
@@ -176,6 +176,7 @@ def tile_listephenswindowforwardimputation_x1_kernel(tc, obs, typed, rho, g, alt
         z_codes = {}
         z_scales = {}
         o_bank = {}
+        product = {}
 
         def live(i):
             return 0 <= i < TILES
@@ -222,11 +223,17 @@ def tile_listephenswindowforwardimputation_x1_kernel(tc, obs, typed, rho, g, alt
 
         def normalize(i):
             post[i] = work.tile([P, H], F32, name="post", tag="post", bufs=5)
-            nc.scalar.activation(out=post[i][:], in_=weight[i][:], func=ACT.Copy, scale=inv_total[i][:])
+            if i < TILES - 1:
+                nc.gpsimd.tensor_scalar(out=post[i][:], in0=weight[i][:], scalar1=inv_total[i][:], scalar2=0.0,
+                                        op0=ALU.mult, op1=ALU.add)
+            else:
+                nc.vector.tensor_scalar(out=post[i][:, :BANK], in0=weight[i][:, :BANK], scalar1=inv_total[i][:], scalar2=None,
+                                        op0=ALU.mult)
+                nc.scalar.activation(out=post[i][:, BANK:], in_=weight[i][:, BANK:], func=ACT.Copy, scale=inv_total[i][:])
 
-        def turn_posterior(i):
+        def turn_posterior(i, tag):
             for grp in range(GROUPS):
-                bank = psum.tile([P, PACK, P], F32, name="z_bank", tag="z")
+                bank = psum.tile([P, PACK, P], F32, name="z_bank", tag=tag)
                 for t in range(PACK):
                     c0 = grp * BANK + t * P
                     nc.tensor.transpose(bank[:, t, :], post[i][:, c0:c0 + P], ident[:])
@@ -259,11 +266,18 @@ def tile_listephenswindowforwardimputation_x1_kernel(tc, obs, typed, rho, g, alt
                                     start=(grp == 0), stop=(grp == GROUPS - 1))
             o_bank[(i, sites.start)] = bank
 
+        def drain_product(i):
+            product[i] = work.tile([P, U], F32, name="product", tag="product")
+            nc.scalar.copy(out=product[i][:], in_=o_bank[(i, 0)][:])
+
         def add_base(i, sites):
             w, t = divmod(i, PACK)
             if w not in out32:
                 out32[w] = work.tile([P, PACK, U], F32, name="out32", tag="out32")
-            nc.vector.tensor_tensor(out=out32[w][:, t, sites], in0=o_bank[(i, sites.start)][:], in1=base_bc[:, w, sites], op=ALU.add)
+            if i in product:
+                nc.gpsimd.tensor_tensor(out=out32[w][:, t, sites], in0=product[i][:], in1=base_bc[:, w, sites], op=ALU.add)
+            else:
+                nc.vector.tensor_tensor(out=out32[w][:, t, sites], in0=o_bank[(i, sites.start)][:], in1=base_bc[:, w, sites], op=ALU.add)
             nc.sync.dma_start(out=out_0[w].rearrange("(p t) u -> p t u", t=PACK)[:, t, sites], in_=out32[w][:, t, sites])
 
         head = [("rows", 0, OBS, 0), ("rows", 0, 0, 0), ("rows", 0, 0, 1), ("rows", 0, 1, 0), ("rows", 0, 1, 1)]
@@ -276,50 +290,69 @@ def tile_listephenswindowforwardimputation_x1_kernel(tc, obs, typed, rho, g, alt
         emissions(0)
         late = ("rows", 0, OBS, 1)
         turn(late, "o")
-        stage(late, on_vector=False)
-        for j in range(2):
-            stage(("alt", 0, 0, j), on_vector=False)
-        pending = [late, ("alt", 0, 0, 0), ("alt", 0, 0, 1)]
+        carried = [late, ("alt", 0, 0, 0)]
+        pending = carried
         every_site = slice(0, U)
 
-        for s in range(TILES + 1):
+        for s in range(TILES):
             now = pieces(s)
-            if live(s - 1) and s - 1 >= PACK:
-                recombine(s - 1)
-            if live(s):
-                row_max(s, 0)
+            if live(s - 3):
+                drain_product(s - 3)
+            for piece in carried:
+                stage(piece, on_vector=False)
             if live(s - 1):
-                invert(s - 1)
                 normalize(s - 1)
-            if live(s - 2):
-                gate(s - 2, 0)
-            if live(s):
-                row_max(s, 1)
-                exponentiate(s)
-            if live(s - 2):
-                gate(s - 2, 1)
-            if s == 0:
-                constants()
-            for piece in pending:
-                quantize(piece)
             if live(s - 3):
                 add_base(s - 3, every_site)
+            row_max(s, 0)
             if live(s - 2):
-                quantize_z(s - 2, 1)
-            if live(s - 1):
-                turn_posterior(s - 1)
-            for piece in now:
-                turn(piece, "in")
+                gate(s - 2, 0)
+            row_max(s, 1)
+            exponentiate(s)
             if live(s + 1):
                 emissions(s + 1)
             if live(s - 2):
-                impute(s - 2, every_site, "o")
+                gate(s - 2, 1)
+            if s == 1:
+                constants()
+            for piece in pending[:1]:
+                quantize(piece)
+            if live(s - 2):
+                quantize_z(s - 2, 1)
+            for piece in pending[1:-1]:
+                quantize(piece)
+            if s >= PACK:
+                recombine(s)
+            for piece in pending[1:][-1:]:
+                quantize(piece)
+            invert(s)
+            if s == 0:
+                for piece in pieces(-1):
+                    turn(piece, "o")
             for piece in now:
-                stage(piece, on_vector=False)
-            pending = now
-        store_scales(range(0, W - 1), [nc.sync])
+                turn(piece, "in")
+            if live(s - 1):
+                turn_posterior(s - 1, "z")
+            if live(s - 2):
+                impute(s - 2, every_site, "o")
+            pending = (pieces(-1) if s == 0 else []) + now
+            carried = [piece for piece in now[-1:] if piece[0] == "rows"]
+            for piece in pending:
+                if piece not in carried:
+                    stage(piece, on_vector=False)
 
         last = TILES - 1
+        normalize(last)
+        drain_product(last - 2)
+        add_base(last - 2, every_site)
+        turn_posterior(last, "in")
+        for grp in range(GROUPS):
+            gate(last - 1, grp)
+        for piece in pending:
+            quantize(piece)
+        store_scales(range(0, W - 1), [nc.sync])
+        quantize_z(last - 1, 1)
+        impute(last - 1, every_site, "o")
         halves = [slice(0, HALF), slice(HALF, U)]
         for grp in range(GROUPS):
             gate(last, grp)

@@ -1,4 +1,5 @@
 from contextlib import ExitStack
+from functools import partial
 
 import concourse.mybir as mybir
 from concourse.masks import make_identity
@@ -21,7 +22,12 @@ BANK = 512
 GROUPS = H // BANK
 HALF = 256
 TILES = W * PACK
-TINY = 2.0 ** -40
+TINY = 2.0 ** -30
+GPSIMD_COLS = 512
+LAG = 3
+NV = 2
+DIRECT = 11
+EARLY = 3
 
 
 def tile_listephenswindowforwardimputation_x1_kernel(tc, obs, typed, rho, g, alt, base, out_0, out_1, out_2):
@@ -79,17 +85,20 @@ def tile_listephenswindowforwardimputation_x1_kernel(tc, obs, typed, rho, g, alt
         g_scaled = keep.tile([P, GROUPS, PACK], F32, name="g_scaled")
         shift = keep.tile([P, W - 1], F32, name="shift")
 
+        safe = keep.tile([P, W - 1], F32, name="safe")
+        inv = keep.tile([P, W - 1], F32, name="inv")
+
         def constants():
-            nc.vector.tensor_scalar(out=g_scaled[:], in0=g_raw[:], scalar1=float(H), scalar2=None, op0=ALU.mult)
+            nc.gpsimd.tensor_scalar(out=g_scaled[:], in0=g_raw[:], scalar1=float(H), scalar2=0.0, op0=ALU.mult, op1=ALU.add)
             stay = keep.tile([P, W - 1], F32, name="stay")
-            nc.vector.tensor_scalar(out=stay[:], in0=rho_raw[:], scalar1=-1.0, scalar2=1.0, op0=ALU.mult, op1=ALU.add)
+            nc.gpsimd.tensor_scalar(out=stay[:], in0=rho_raw[:], scalar1=-float(H), scalar2=float(H), op0=ALU.mult, op1=ALU.add)
             guard = keep.tile([P, W - 1], F32, name="guard")
-            nc.vector.tensor_scalar(out=guard[:], in0=stay[:], scalar1=0.0, scalar2=TINY, op0=ALU.is_equal, op1=ALU.mult)
-            safe = keep.tile([P, W - 1], F32, name="safe")
-            nc.vector.tensor_tensor(out=safe[:], in0=stay[:], in1=guard[:], op=ALU.add)
-            inv = keep.tile([P, W - 1], F32, name="inv")
+            nc.gpsimd.tensor_scalar(out=guard[:], in0=stay[:], scalar1=0.0, scalar2=TINY, op0=ALU.is_equal, op1=ALU.mult)
+            nc.gpsimd.tensor_tensor(out=safe[:], in0=stay[:], in1=guard[:], op=ALU.add)
+
+        def shifts():
             nc.vector.reciprocal(out=inv[:], in_=safe[:])
-            nc.vector.scalar_tensor_tensor(out=shift[:], in0=rho_raw[:], scalar=1.0 / H, in1=inv[:], op0=ALU.mult, op1=ALU.mult)
+            nc.gpsimd.tensor_tensor(out=shift[:], in0=rho_raw[:], in1=inv[:], op=ALU.mult)
 
         codes = {}
         scales = {}
@@ -123,9 +132,12 @@ def tile_listephenswindowforwardimputation_x1_kernel(tc, obs, typed, rho, g, alt
                      in_=banks[piece][:].rearrange("p (s u) m -> p s m u", u=2))
             else:
                 src = alt_raw[(w, part)] if kind == "alt" else out32[w]
-                copy(out=st[:].rearrange("p (u t) -> p u t", t=PACK),
-                     in_=src[:, :, j * HALF:(j + 1) * HALF].rearrange("p t u -> p u t"))
+                copy(out=st[:].rearrange("p (c i t) -> p c t i", i=4, t=PACK),
+                     in_=src[:, :, j * HALF:(j + 1) * HALF].rearrange("p t (c i) -> p c t i", i=4))
             staged[piece] = st
+
+        def last_half(w):
+            return 1 if w < W - 1 else 0
 
         def quantize(piece):
             kind, w, part, j = piece
@@ -143,6 +155,12 @@ def tile_listephenswindowforwardimputation_x1_kernel(tc, obs, typed, rho, g, alt
             nc.vector.quantize_mx(out=c[:, cols].bitcast(FP8X4), scales=s[:, cols], in_=staged[piece][:])
             if kind == "out":
                 nc.sync.dma_start(out=words_hbm[:, cols], in_=out_codes[:, cols].bitcast(I32))
+                if j == last_half(w) and w >= W - 2:
+                    store_scales(range(0, w + 1) if w < W - 1 else range(w, W), [nc.sync] if w < W - 1 else [nc.sync, nc.scalar])
+
+        def store_words(w):
+            cols = slice(w * U, (w + 1) * U)
+            nc.sync.dma_start(out=words_hbm[:, cols], in_=out_codes[:, cols].bitcast(I32))
 
         def store_scales(windows, queues):
             cols = slice(windows.start * U // 4, windows.stop * U // 4)
@@ -155,9 +173,11 @@ def tile_listephenswindowforwardimputation_x1_kernel(tc, obs, typed, rho, g, alt
             w, r = divmod(step + 2, PACK)
             if 0 <= w < W:
                 found.append(("alt", w, r // 2, r % 2))
-            w, r = divmod(step - 6, PACK)
-            if 0 <= w < W - 1 and r < 2:
+            w, r = divmod(step - 7, PACK)
+            if 0 <= w < W - 2 and r < 2:
                 found.append(("out", w, 0, r))
+            if step == DIRECT + 3:
+                found.extend([("out", W - 2, 0, 0), ("out", W - 2, 0, 1)])
             w, r = divmod(step + 5, PACK)
             if 1 <= w < W:
                 first, stop = [(0, 1), (1, 3), (3, 5), (5, 6)][r]
@@ -181,10 +201,10 @@ def tile_listephenswindowforwardimputation_x1_kernel(tc, obs, typed, rho, g, alt
         def live(i):
             return 0 <= i < TILES
 
-        def emissions(i):
+        def emissions(i, groups=range(GROUPS)):
             w, t = divmod(i, PACK)
             cols = slice(t * P, (t + 1) * P)
-            for grp in range(GROUPS):
+            for grp in groups:
                 bank = psum.tile([P, BANK], F32, name="e_bank", tag="e")
                 nc.tensor.matmul_mx(out=bank[:], lhsT=codes[("rows", w, OBS)][:, cols].bitcast(FP8X4),
                                     lhsT_scale=scales[("rows", w, OBS)][:, cols],
@@ -223,13 +243,11 @@ def tile_listephenswindowforwardimputation_x1_kernel(tc, obs, typed, rho, g, alt
 
         def normalize(i):
             post[i] = work.tile([P, H], F32, name="post", tag="post", bufs=5)
-            if i < TILES - 1:
-                nc.gpsimd.tensor_scalar(out=post[i][:], in0=weight[i][:], scalar1=inv_total[i][:], scalar2=0.0,
-                                        op0=ALU.mult, op1=ALU.add)
-            else:
-                nc.vector.tensor_scalar(out=post[i][:, :BANK], in0=weight[i][:, :BANK], scalar1=inv_total[i][:], scalar2=None,
-                                        op0=ALU.mult)
-                nc.scalar.activation(out=post[i][:, BANK:], in_=weight[i][:, BANK:], func=ACT.Copy, scale=inv_total[i][:])
+            split = BANK if i == TILES - 1 else (H if i < EARLY or i > DIRECT + 2 else GPSIMD_COLS)
+            nc.gpsimd.tensor_scalar(out=post[i][:, :split], in0=weight[i][:, :split], scalar1=inv_total[i][:], scalar2=0.0,
+                                    op0=ALU.mult, op1=ALU.add)
+            if split < H:
+                nc.scalar.activation(out=post[i][:, split:], in_=weight[i][:, split:], func=ACT.Copy, scale=inv_total[i][:])
 
         def turn_posterior(i, tag):
             for grp in range(GROUPS):
@@ -278,7 +296,8 @@ def tile_listephenswindowforwardimputation_x1_kernel(tc, obs, typed, rho, g, alt
                 nc.gpsimd.tensor_tensor(out=out32[w][:, t, sites], in0=product[i][:], in1=base_bc[:, w, sites], op=ALU.add)
             else:
                 nc.vector.tensor_tensor(out=out32[w][:, t, sites], in0=o_bank[(i, sites.start)][:], in1=base_bc[:, w, sites], op=ALU.add)
-            nc.sync.dma_start(out=out_0[w].rearrange("(p t) u -> p t u", t=PACK)[:, t, sites], in_=out32[w][:, t, sites])
+            if sites.stop == U:
+                nc.sync.dma_start(out=out_0[w].rearrange("(p t) u -> p t u", t=PACK)[:, t, :], in_=out32[w][:, t, :])
 
         head = [("rows", 0, OBS, 0), ("rows", 0, 0, 0), ("rows", 0, 0, 1), ("rows", 0, 1, 0), ("rows", 0, 1, 1)]
         for piece, tag in zip(head, ["in", "in", "z", "z", "o"]):
@@ -287,83 +306,102 @@ def tile_listephenswindowforwardimputation_x1_kernel(tc, obs, typed, rho, g, alt
             stage(piece, on_vector=(n == 1))
         for piece in head:
             quantize(piece)
-        emissions(0)
         late = ("rows", 0, OBS, 1)
+        emissions(0)
         turn(late, "o")
-        carried = [late, ("alt", 0, 0, 0)]
-        pending = carried
+        carried = [late]
+        pending = [("alt", 0, 0, 0), late]
         every_site = slice(0, U)
+
+        def on_vector(piece):
+            return piece[0] == "alt" and piece[1] == 0 and piece[2] * 2 + piece[3] < NV
 
         for s in range(TILES):
             now = pieces(s)
-            if live(s - 3):
-                drain_product(s - 3)
+            if s > LAG:
+                normalize(s - 1)
             for piece in carried:
                 stage(piece, on_vector=False)
-            if live(s - 1):
-                normalize(s - 1)
-            if live(s - 3):
-                add_base(s - 3, every_site)
             row_max(s, 0)
+            if 0 < s <= LAG:
+                invert(s - 1)
+                normalize(s - 1)
+            if s - 4 in product:
+                add_base(s - 4, every_site)
             if live(s - 2):
                 gate(s - 2, 0)
             row_max(s, 1)
             exponentiate(s)
+            if 0 <= s - 3 < DIRECT:
+                drain_product(s - 3)
             if live(s + 1):
                 emissions(s + 1)
             if live(s - 2):
                 gate(s - 2, 1)
-            if s == 1:
+            if s == 0:
                 constants()
-            for piece in pending[:1]:
-                quantize(piece)
+            if s == 2:
+                shifts()
+            for piece in pending:
+                if on_vector(piece):
+                    stage(piece, on_vector=True)
+            fillers = [partial(quantize, piece) for piece in sorted(pending, key=on_vector)]
+            if s - 3 >= DIRECT:
+                fillers.insert(0, partial(add_base, s - 3, every_site))
+            for job in fillers[:1]:
+                job()
             if live(s - 2):
                 quantize_z(s - 2, 1)
-            for piece in pending[1:-1]:
-                quantize(piece)
+            for job in fillers[1:-1]:
+                job()
             if s >= PACK:
                 recombine(s)
-            for piece in pending[1:][-1:]:
-                quantize(piece)
-            invert(s)
+            for job in fillers[1:][-1:]:
+                job()
+            if s >= LAG:
+                invert(s)
             if s == 0:
                 for piece in pieces(-1):
                     turn(piece, "o")
-            for piece in now:
-                turn(piece, "in")
             if live(s - 1):
                 turn_posterior(s - 1, "z")
+            for piece in now:
+                turn(piece, "in")
             if live(s - 2):
                 impute(s - 2, every_site, "o")
             pending = (pieces(-1) if s == 0 else []) + now
-            carried = [piece for piece in now[-1:] if piece[0] == "rows"]
+            carried = [piece for piece in now if piece[0] == "rows"]
             for piece in pending:
-                if piece not in carried:
+                if piece not in carried and not on_vector(piece):
                     stage(piece, on_vector=False)
 
         last = TILES - 1
         normalize(last)
-        drain_product(last - 2)
-        add_base(last - 2, every_site)
         turn_posterior(last, "in")
         for grp in range(GROUPS):
             gate(last - 1, grp)
-        for piece in pending:
-            quantize(piece)
-        store_scales(range(0, W - 1), [nc.sync])
+        add_base(last - 2, every_site)
         quantize_z(last - 1, 1)
         impute(last - 1, every_site, "o")
-        halves = [slice(0, HALF), slice(HALF, U)]
         for grp in range(GROUPS):
             gate(last, grp)
         quantize_z(last, GROUPS)
         add_base(last - 1, every_site)
-        for sites in halves:
-            impute(last, sites, "e")
-        for sites in halves:
+        quarters = [slice(n * P, (n + 1) * P) for n in range(4)]
+        for sites, tag in zip(quarters, ["e", "e", "z", "z"]):
+            impute(last, sites, tag)
+        for sites in quarters:
             add_base(last, sites)
-        for j in range(2):
-            stage(("out", W - 1, 0, j), on_vector=(j == 1))
-        for j in (1, 0):
-            quantize(("out", W - 1, 0, j))
-        store_scales(range(W - 1, W), [nc.sync, nc.scalar])
+        final = work.tile([P, PACK * U], BF16, name="final", tag="final", bufs=1, align_bytes=64)
+        w = W - 1
+        for n in range(4):
+            copy = nc.scalar.copy if n < 2 else nc.vector.tensor_copy
+            copy(out=final[:, n * BANK:(n + 1) * BANK].rearrange("p (c i t) -> p c t i", i=4, t=PACK),
+                 in_=out32[w][:, :, quarters[n]].rearrange("p t (c i) -> p c t i", i=4))
+        for n in (0, 2, 3, 1):
+            cols = slice(w * U + n * P, w * U + (n + 1) * P)
+            nc.vector.quantize_mx(out=out_codes[:, cols].bitcast(FP8X4), scales=out_scales[:, cols], in_=final[:, n * BANK:(n + 1) * BANK])
+            if n % 2 == 1:
+                cols = slice(w * U + (n - 1) * P, w * U + (n + 1) * P)
+                nc.sync.dma_start(out=words_hbm[:, cols], in_=out_codes[:, cols].bitcast(I32))
+        store_scales(range(w, W), [nc.sync, nc.scalar])

@@ -19,15 +19,38 @@ ACT = mybir.ActivationFunctionType
 P = 128
 PACK = 4
 BANK = 512
-GROUPS = H // BANK
+PASSES = H // BANK
+OBS = PASSES
 HALF = 256
+RUN = 4
 TILES = W * PACK
+LAST = TILES - 1
 TINY = 2.0 ** -30
+
 GPSIMD_COLS = 512
-LAG = 3
-NV = 2
 DIRECT = 11
-EARLY = 3
+LAG = 3
+MAX_PIECES, MAX_LONG = 3, 2
+
+
+def piece_schedule():
+    schedule = {step: [] for step in range(-1, TILES)}
+    for w in range(W):
+        for n in range(2 * PASSES):
+            if PACK * w - 2 + n >= 0:
+                schedule[PACK * w - 2 + n].append(("alt", w, n // 2, n % 2))
+    rows = {step: [] for step in schedule}
+    for w in range(1, W):
+        for n in range(2 * (PASSES + 1)):
+            rows[PACK * w - 5 + (n + 1) // 2].append(("rows", w, n // 2, n % 2))
+    for w in range(W - 1):
+        closing = PACK * w + PACK - 1
+        step = closing + (3 if closing >= DIRECT else 4)
+        for half in range(2):
+            while len(schedule[step]) + len(rows[step]) >= MAX_PIECES or len(schedule[step]) >= MAX_LONG:
+                step = step + 1
+            schedule[step].append(("out", w, 0, half))
+    return {step: schedule[step] + rows[step] for step in schedule}
 
 
 def tile_listephenswindowforwardimputation_x1_kernel(tc, obs, typed, rho, g, alt, base, out_0, out_1, out_2):
@@ -44,37 +67,37 @@ def tile_listephenswindowforwardimputation_x1_kernel(tc, obs, typed, rho, g, alt
         rows_raw = {}
         alt_raw = {}
 
-        def load_rows(w, part, j):
-            src = obs[w] if part == GROUPS else typed[w, part * BANK:(part + 1) * BANK, :]
-            raw = keep.tile([P, 2, T], BF16, name="rows_%d_%d_%d" % (w, part, j))
-            nc.sync.dma_start(out=raw[:], in_=src.rearrange("(m t) k -> m t k", t=PACK)[:, 2 * j:2 * j + 2, :])
-            rows_raw[(w, part, j)] = raw
+        def load_rows(w, part, half):
+            src = obs[w] if part == OBS else typed[w, part * BANK:(part + 1) * BANK, :]
+            raw = keep.tile([P, 2, T], BF16, name="rows_%d_%d_%d" % (w, part, half))
+            nc.sync.dma_start(out=raw[:], in_=src.rearrange("(m t) k -> m t k", t=PACK)[:, 2 * half:2 * half + 2, :])
+            rows_raw[(w, part, half)] = raw
 
-        def load_alt(w, grp):
-            raw = keep.tile([P, PACK, U], BF16, name="alt_%d_%d" % (w, grp))
-            nc.sync.dma_start(out=raw[:], in_=alt[w, grp * BANK:(grp + 1) * BANK, :].rearrange("(p j) u -> p j u", j=PACK))
-            alt_raw[(w, grp)] = raw
+        def load_alt(w, a):
+            raw = keep.tile([P, PACK, U], BF16, name="alt_%d_%d" % (w, a))
+            nc.sync.dma_start(out=raw[:], in_=alt[w, a * BANK:(a + 1) * BANK, :].rearrange("(p t) u -> p t u", t=PACK))
+            alt_raw[(w, a)] = raw
 
-        OBS = GROUPS
-        g_raw = keep.tile([P, GROUPS, PACK], BF16, name="g_raw")
+        g_raw = keep.tile([P, PASSES, PACK], BF16, name="g_raw")
         rho_raw = keep.tile([P, W - 1], BF16, name="rho_raw")
-        base_bc = keep.tile([P, W, U], BF16, name="base_bc")
-        for w in range(W):
-            if w == 0:
-                order = [(OBS, 0), (0, 0), (0, 1), (1, 0), (1, 1), (OBS, 1)]
-            else:
-                order = [(0, 0), (0, 1), (1, 0), (1, 1), (OBS, 0), (OBS, 1)][1 if w == 1 else 0:]
-            for part, j in order:
-                load_rows(w, part, j)
-            for grp in range(GROUPS):
-                load_alt(w, grp)
-                if w == 0 and grp == 0:
-                    load_rows(1, 0, 0)
-            if w == 0:
-                nc.sync.dma_start(out=g_raw[:], in_=g.rearrange("(a p t) -> p a t", a=GROUPS, t=PACK))
-                nc.sync.dma_start(out=rho_raw[:], in_=rho.partition_broadcast(P))
+        base_rows = keep.tile([P, W, U], BF16, name="base_rows")
+        head = [("rows", 0, OBS, 0), ("rows", 0, 0, 0), ("rows", 0, 0, 1), ("rows", 0, 1, 0), ("rows", 0, 1, 1)]
+        late_obs = ("rows", 0, OBS, 1)
+        for piece in head + [late_obs]:
+            load_rows(*piece[1:])
+        load_alt(0, 0)
+        load_rows(1, 0, 0)
+        load_alt(0, 1)
+        nc.sync.dma_start(out=g_raw[:], in_=g.rearrange("(a p t) -> p a t", a=PASSES, t=PACK))
+        nc.sync.dma_start(out=rho_raw[:], in_=rho.partition_broadcast(P))
+        for w in range(1, W):
+            for n in range(2 * (PASSES + 1)):
+                if (w, n // 2, n % 2) not in rows_raw:
+                    load_rows(w, n // 2, n % 2)
+            for a in range(PASSES):
+                load_alt(w, a)
             if w == 1:
-                nc.sync.dma_start(out=base_bc[:].rearrange("p w u -> p (w u)"),
+                nc.sync.dma_start(out=base_rows[:].rearrange("p w u -> p (w u)"),
                                   in_=base.rearrange("w u -> (w u)").partition_broadcast(P))
 
         out_codes = keep.tile([P, W * U], U32, name="out_codes", align_bytes=64)
@@ -82,107 +105,79 @@ def tile_listephenswindowforwardimputation_x1_kernel(tc, obs, typed, rho, g, alt
         words_hbm = out_1[0].rearrange("p m t -> p (m t)").bitcast(I32)
         scales_hbm = out_2[0].bitcast(I32)
 
-        g_scaled = keep.tile([P, GROUPS, PACK], F32, name="g_scaled")
+        def store_words(cols):
+            nc.sync.dma_start(out=words_hbm[:, cols], in_=out_codes[:, cols].bitcast(I32))
+
+        def store_scales(windows, queues):
+            cols = slice(windows.start * U // 4, windows.stop * U // 4)
+            for n in range(4):
+                queues[n % len(queues)].dma_start(out=scales_hbm[4 * n:4 * n + 4, cols],
+                                                  in_=out_scales[32 * n:32 * n + 4, :].bitcast(I32)[:, cols])
+
+        g_scaled = keep.tile([P, PASSES, PACK], F32, name="g_scaled")
         shift = keep.tile([P, W - 1], F32, name="shift")
+        divisor = keep.tile([P, W - 1], F32, name="divisor")
+        inv_divisor = keep.tile([P, W - 1], F32, name="inv_divisor")
 
-        safe = keep.tile([P, W - 1], F32, name="safe")
-        inv = keep.tile([P, W - 1], F32, name="inv")
-
-        def constants():
+        def make_divisor():
             nc.gpsimd.tensor_scalar(out=g_scaled[:], in0=g_raw[:], scalar1=float(H), scalar2=0.0, op0=ALU.mult, op1=ALU.add)
             stay = keep.tile([P, W - 1], F32, name="stay")
             nc.gpsimd.tensor_scalar(out=stay[:], in0=rho_raw[:], scalar1=-float(H), scalar2=float(H), op0=ALU.mult, op1=ALU.add)
             guard = keep.tile([P, W - 1], F32, name="guard")
             nc.gpsimd.tensor_scalar(out=guard[:], in0=stay[:], scalar1=0.0, scalar2=TINY, op0=ALU.is_equal, op1=ALU.mult)
-            nc.gpsimd.tensor_tensor(out=safe[:], in0=stay[:], in1=guard[:], op=ALU.add)
+            nc.gpsimd.tensor_tensor(out=divisor[:], in0=stay[:], in1=guard[:], op=ALU.add)
 
-        def shifts():
-            nc.vector.reciprocal(out=inv[:], in_=safe[:])
-            nc.gpsimd.tensor_tensor(out=shift[:], in0=rho_raw[:], in1=inv[:], op=ALU.mult)
+        def make_shift():
+            nc.vector.reciprocal(out=inv_divisor[:], in_=divisor[:])
+            nc.gpsimd.tensor_tensor(out=shift[:], in0=rho_raw[:], in1=inv_divisor[:], op=ALU.mult)
 
         codes = {}
         scales = {}
-        banks = {}
+        turned = {}
         staged = {}
         out32 = {}
 
-        def planes(key, tag, bufs):
-            if key not in codes:
-                codes[key] = work.tile([P, BANK], U32, name="c_" + tag, tag="c_" + tag, bufs=bufs, align_bytes=64)
-                scales[key] = work.tile([P, BANK], U8, name="s_" + tag, tag="s_" + tag, bufs=bufs, align_bytes=64)
-            return codes[key], scales[key]
-
         def turn(piece, tag):
-            kind, w, part, j = piece
+            kind, w, part, half = piece
             if kind != "rows":
                 return
-            bank = psum.tile([P, PACK, P], F32, name="bank_" + tag, tag=tag)
-            words = rows_raw[(w, part, j)][:].bitcast(F32)
+            bank = psum.tile([P, PACK, P], F32, name="turned", tag=tag)
+            words = rows_raw[(w, part, half)][:].bitcast(F32)
             for s in range(2):
                 for u in range(2):
                     nc.tensor.transpose(bank[:, 2 * s + u, :], words[:, s, u:T // 2:2], ident[:])
-            banks[piece] = bank
+            turned[piece] = bank
 
-        def stage(piece, on_vector):
-            kind, w, part, j = piece
-            copy = nc.vector.tensor_copy if on_vector else nc.scalar.copy
-            st = work.tile([P, PACK * HALF], BF16, name="staged", tag="staged", bufs=6, align_bytes=64)
+        def interleave(copy, dst, src):
+            copy(out=dst.rearrange("p (c i t) -> p c t i", i=RUN, t=PACK), in_=src.rearrange("p t (c i) -> p c t i", i=RUN))
+
+        def lay_out(piece, copy):
+            kind, w, part, half = piece
+            laid = work.tile([P, PACK * HALF], BF16, name="staged", tag="staged", bufs=6, align_bytes=64)
             if kind == "rows":
-                copy(out=st[:].bitcast(F32).rearrange("p (s m u) -> p s m u", s=2, u=2),
-                     in_=banks[piece][:].rearrange("p (s u) m -> p s m u", u=2))
+                copy(out=laid[:].bitcast(F32).rearrange("p (s m u) -> p s m u", s=2, u=2),
+                     in_=turned[piece][:].rearrange("p (s u) m -> p s m u", u=2))
             else:
                 src = alt_raw[(w, part)] if kind == "alt" else out32[w]
-                copy(out=st[:].rearrange("p (c i t) -> p c t i", i=4, t=PACK),
-                     in_=src[:, :, j * HALF:(j + 1) * HALF].rearrange("p t (c i) -> p c t i", i=4))
-            staged[piece] = st
-
-        def last_half(w):
-            return 1 if w < W - 1 else 0
+                interleave(copy, laid[:], src[:, :, half * HALF:(half + 1) * HALF])
+            staged[piece] = laid
 
         def quantize(piece):
-            kind, w, part, j = piece
+            kind, w, part, half = piece
             if kind == "out":
-                cols = slice(w * U + j * HALF, w * U + (j + 1) * HALF)
-                c, s = out_codes, out_scales
-            else:
-                cols = slice(j * HALF, (j + 1) * HALF)
-                if kind == "alt":
-                    c, s = planes((kind, w, part), "alt", 4)
-                elif part == OBS:
-                    c, s = planes((kind, w, part), "obs", 2)
-                else:
-                    c, s = planes((kind, w, part), "typed", 4)
-            nc.vector.quantize_mx(out=c[:, cols].bitcast(FP8X4), scales=s[:, cols], in_=staged[piece][:])
-            if kind == "out":
-                nc.sync.dma_start(out=words_hbm[:, cols], in_=out_codes[:, cols].bitcast(I32))
-                if j == last_half(w) and w >= W - 2:
-                    store_scales(range(0, w + 1) if w < W - 1 else range(w, W), [nc.sync] if w < W - 1 else [nc.sync, nc.scalar])
-
-        def store_words(w):
-            cols = slice(w * U, (w + 1) * U)
-            nc.sync.dma_start(out=words_hbm[:, cols], in_=out_codes[:, cols].bitcast(I32))
-
-        def store_scales(windows, queues):
-            cols = slice(windows.start * U // 4, windows.stop * U // 4)
-            for quad in range(4):
-                queues[quad % len(queues)].dma_start(out=scales_hbm[4 * quad:4 * quad + 4, cols],
-                                                     in_=out_scales[32 * quad:32 * quad + 4, :].bitcast(I32)[:, cols])
-
-        def pieces(step):
-            found = []
-            w, r = divmod(step + 2, PACK)
-            if 0 <= w < W:
-                found.append(("alt", w, r // 2, r % 2))
-            w, r = divmod(step - 7, PACK)
-            if 0 <= w < W - 2 and r < 2:
-                found.append(("out", w, 0, r))
-            if step == DIRECT + 3:
-                found.extend([("out", W - 2, 0, 0), ("out", W - 2, 0, 1)])
-            w, r = divmod(step + 5, PACK)
-            if 1 <= w < W:
-                first, stop = [(0, 1), (1, 3), (3, 5), (5, 6)][r]
-                found.extend([("rows", w, n // 2, n % 2) for n in range(first, stop)])
-            return found
+                cols = slice(w * U + half * HALF, w * U + (half + 1) * HALF)
+                nc.vector.quantize_mx(out=out_codes[:, cols].bitcast(FP8X4), scales=out_scales[:, cols], in_=staged[piece][:])
+                store_words(cols)
+                if (w, half) == (W - 2, 1):
+                    store_scales(range(0, W - 1), [nc.sync])
+                return
+            key = (kind, w, part)
+            if key not in codes:
+                tag, bufs = ("alt", 2 * PASSES) if kind == "alt" else (("obs", 2) if part == OBS else ("typed", 2 * PASSES))
+                codes[key] = work.tile([P, BANK], U32, name="c_" + tag, tag="c_" + tag, bufs=bufs, align_bytes=64)
+                scales[key] = work.tile([P, BANK], U8, name="s_" + tag, tag="s_" + tag, bufs=bufs, align_bytes=64)
+            cols = slice(half * HALF, (half + 1) * HALF)
+            nc.vector.quantize_mx(out=codes[key][:, cols].bitcast(FP8X4), scales=scales[key][:, cols], in_=staged[piece][:])
 
         e_bank = {}
         neg_e = {}
@@ -191,43 +186,40 @@ def tile_listephenswindowforwardimputation_x1_kernel(tc, obs, typed, rho, g, alt
         total = {}
         inv_total = {}
         post = {}
-        z_bank = {}
+        post_turned = {}
         z_bf = {}
         z_codes = {}
         z_scales = {}
         o_bank = {}
         product = {}
 
-        def live(i):
-            return 0 <= i < TILES
-
-        def emissions(i, groups=range(GROUPS)):
+        def emissions(i):
             w, t = divmod(i, PACK)
             cols = slice(t * P, (t + 1) * P)
-            for grp in groups:
+            for a in range(PASSES):
                 bank = psum.tile([P, BANK], F32, name="e_bank", tag="e")
                 nc.tensor.matmul_mx(out=bank[:], lhsT=codes[("rows", w, OBS)][:, cols].bitcast(FP8X4),
                                     lhsT_scale=scales[("rows", w, OBS)][:, cols],
-                                    rhs=codes[("rows", w, grp)][:].bitcast(FP8X4), rhs_scale=scales[("rows", w, grp)][:],
+                                    rhs=codes[("rows", w, a)][:].bitcast(FP8X4), rhs_scale=scales[("rows", w, a)][:],
                                     start=True, stop=True)
-                e_bank[(i, grp)] = bank
+                e_bank[(i, a)] = bank
 
-        def row_max(i, grp):
-            if grp == 0:
+        def row_max(i, a):
+            if a == 0:
                 neg_e[i] = work.tile([P, H], F32, name="neg_e", tag="neg_e")
-            m = work.tile([P, 1], F32, name="neg_max", tag="neg_max", bufs=4)
-            nc.vector.tensor_scalar(out=neg_e[i][:, grp * BANK:(grp + 1) * BANK], in0=e_bank[(i, grp)][:], scalar1=-1.0,
-                                    scalar2=neg_max[i][:] if grp else None, op0=ALU.mult, op1=ALU.min, accum_out=m[:])
-            neg_max[i] = m
+            least = work.tile([P, 1], F32, name="neg_max", tag="neg_max", bufs=4)
+            nc.vector.tensor_scalar(out=neg_e[i][:, a * BANK:(a + 1) * BANK], in0=e_bank[(i, a)][:], scalar1=-1.0,
+                                    scalar2=neg_max[i][:] if a else None, op0=ALU.mult, op1=ALU.min, accum_out=least[:])
+            neg_max[i] = least
 
         def exponentiate(i):
-            x = work.tile([P, H], F32, name="x", tag="x")
+            weight[i] = work.tile([P, H], F32, name="x", tag="x")
             if i < PACK:
                 total[i] = work.tile([P, 1], F32, name="total", tag="total")
-                nc.scalar.activation(out=x[:], in_=neg_e[i][:], func=ACT.Exp, bias=neg_max[i][:], scale=-1.0, accum_out=total[i][:])
+                nc.scalar.activation(out=weight[i][:], in_=neg_e[i][:], func=ACT.Exp, bias=neg_max[i][:], scale=-1.0,
+                                     accum_out=total[i][:])
             else:
-                nc.scalar.activation(out=x[:], in_=neg_e[i][:], func=ACT.Exp, bias=neg_max[i][:], scale=-1.0)
-            weight[i] = x
+                nc.scalar.activation(out=weight[i][:], in_=neg_e[i][:], func=ACT.Exp, bias=neg_max[i][:], scale=-1.0)
 
         def recombine(i):
             w = i // PACK
@@ -242,33 +234,34 @@ def tile_listephenswindowforwardimputation_x1_kernel(tc, obs, typed, rho, g, alt
             nc.vector.reciprocal(out=inv_total[i][:], in_=total[i][:])
 
         def normalize(i):
-            post[i] = work.tile([P, H], F32, name="post", tag="post", bufs=5)
-            split = BANK if i == TILES - 1 else (H if i < EARLY or i > DIRECT + 2 else GPSIMD_COLS)
+            post[i] = work.tile([P, H], F32, name="post", tag="post", bufs=PACK + 1)
+            alone = i < PACK or DIRECT + 2 < i < LAST
+            split = H if alone else GPSIMD_COLS
             nc.gpsimd.tensor_scalar(out=post[i][:, :split], in0=weight[i][:, :split], scalar1=inv_total[i][:], scalar2=0.0,
                                     op0=ALU.mult, op1=ALU.add)
-            if split < H:
+            if not alone:
                 nc.scalar.activation(out=post[i][:, split:], in_=weight[i][:, split:], func=ACT.Copy, scale=inv_total[i][:])
 
         def turn_posterior(i, tag):
-            for grp in range(GROUPS):
-                bank = psum.tile([P, PACK, P], F32, name="z_bank", tag=tag)
+            for a in range(PASSES):
+                bank = psum.tile([P, PACK, P], F32, name="post_turned", tag=tag)
                 for t in range(PACK):
-                    c0 = grp * BANK + t * P
-                    nc.tensor.transpose(bank[:, t, :], post[i][:, c0:c0 + P], ident[:])
-                z_bank[(i, grp)] = bank
+                    first = a * BANK + t * P
+                    nc.tensor.transpose(bank[:, t, :], post[i][:, first:first + P], ident[:])
+                post_turned[(i, a)] = bank
 
-        def gate(i, grp):
-            if grp == 0:
+        def gate(i, a):
+            if a == 0:
                 z_bf[i] = work.tile([P, H], BF16, name="z_bf", tag="z_bf", align_bytes=64)
             nc.vector.scalar_tensor_tensor(
-                out=z_bf[i][:, grp * BANK:(grp + 1) * BANK].rearrange("p (q t) -> p q t", t=PACK),
-                in0=z_bank[(i, grp)][:].rearrange("p t q -> p q t"), scalar=1.0 / H,
-                in1=g_scaled[:, grp, :].unsqueeze(1).to_broadcast([P, P, PACK]), op0=ALU.subtract, op1=ALU.mult)
+                out=z_bf[i][:, a * BANK:(a + 1) * BANK].rearrange("p (q t) -> p q t", t=PACK),
+                in0=post_turned[(i, a)][:].rearrange("p t q -> p q t"), scalar=1.0 / H,
+                in1=g_scaled[:, a, :].unsqueeze(1).to_broadcast([P, P, PACK]), op0=ALU.subtract, op1=ALU.mult)
 
         def quantize_z(i, parts):
-            z_codes[i] = work.tile([P, GROUPS * P], U32, name="z_codes", tag="z_codes", align_bytes=64)
-            z_scales[i] = work.tile([P, GROUPS * P], U8, name="z_scales", tag="z_scales", align_bytes=64)
-            width = GROUPS * P // parts
+            z_codes[i] = work.tile([P, PASSES * P], U32, name="z_codes", tag="z_codes", align_bytes=64)
+            z_scales[i] = work.tile([P, PASSES * P], U8, name="z_scales", tag="z_scales", align_bytes=64)
+            width = PASSES * P // parts
             for n in range(parts):
                 cols = slice(n * width, (n + 1) * width)
                 nc.vector.quantize_mx(out=z_codes[i][:, cols].bitcast(FP8X4), scales=z_scales[i][:, cols],
@@ -277,11 +270,11 @@ def tile_listephenswindowforwardimputation_x1_kernel(tc, obs, typed, rho, g, alt
         def impute(i, sites, tag):
             w = i // PACK
             bank = psum.tile([P, sites.stop - sites.start], F32, name="o_bank", tag=tag)
-            for grp in range(GROUPS):
-                cols = slice(grp * P, (grp + 1) * P)
+            for a in range(PASSES):
+                cols = slice(a * P, (a + 1) * P)
                 nc.tensor.matmul_mx(out=bank[:], lhsT=z_codes[i][:, cols].bitcast(FP8X4), lhsT_scale=z_scales[i][:, cols],
-                                    rhs=codes[("alt", w, grp)][:, sites].bitcast(FP8X4), rhs_scale=scales[("alt", w, grp)][:, sites],
-                                    start=(grp == 0), stop=(grp == GROUPS - 1))
+                                    rhs=codes[("alt", w, a)][:, sites].bitcast(FP8X4), rhs_scale=scales[("alt", w, a)][:, sites],
+                                    start=(a == 0), stop=(a == PASSES - 1))
             o_bank[(i, sites.start)] = bank
 
         def drain_product(i):
@@ -292,65 +285,60 @@ def tile_listephenswindowforwardimputation_x1_kernel(tc, obs, typed, rho, g, alt
             w, t = divmod(i, PACK)
             if w not in out32:
                 out32[w] = work.tile([P, PACK, U], F32, name="out32", tag="out32")
-            if i in product:
-                nc.gpsimd.tensor_tensor(out=out32[w][:, t, sites], in0=product[i][:], in1=base_bc[:, w, sites], op=ALU.add)
+            if i < DIRECT:
+                nc.gpsimd.tensor_tensor(out=out32[w][:, t, sites], in0=product[i][:], in1=base_rows[:, w, sites], op=ALU.add)
             else:
-                nc.vector.tensor_tensor(out=out32[w][:, t, sites], in0=o_bank[(i, sites.start)][:], in1=base_bc[:, w, sites], op=ALU.add)
+                nc.vector.tensor_tensor(out=out32[w][:, t, sites], in0=o_bank[(i, sites.start)][:], in1=base_rows[:, w, sites],
+                                        op=ALU.add)
             if sites.stop == U:
                 nc.sync.dma_start(out=out_0[w].rearrange("(p t) u -> p t u", t=PACK)[:, t, :], in_=out32[w][:, t, :])
 
-        head = [("rows", 0, OBS, 0), ("rows", 0, 0, 0), ("rows", 0, 0, 1), ("rows", 0, 1, 0), ("rows", 0, 1, 1)]
         for piece, tag in zip(head, ["in", "in", "z", "z", "o"]):
             turn(piece, tag)
         for n, piece in enumerate(head):
-            stage(piece, on_vector=(n == 1))
+            lay_out(piece, nc.vector.tensor_copy if n == 1 else nc.scalar.copy)
         for piece in head:
             quantize(piece)
-        late = ("rows", 0, OBS, 1)
         emissions(0)
-        turn(late, "o")
-        carried = [late]
-        pending = [("alt", 0, 0, 0), late]
+        turn(late_obs, "o")
+
+        schedule = piece_schedule()
         every_site = slice(0, U)
-
-        def on_vector(piece):
-            return piece[0] == "alt" and piece[1] == 0 and piece[2] * 2 + piece[3] < NV
-
+        carried = [("alt", 0, 0, 0), ("alt", 0, 0, 1), late_obs]
+        pending = carried
         for s in range(TILES):
-            now = pieces(s)
             if s > LAG:
                 normalize(s - 1)
             for piece in carried:
-                stage(piece, on_vector=False)
+                lay_out(piece, nc.scalar.copy)
+
             row_max(s, 0)
             if 0 < s <= LAG:
                 invert(s - 1)
                 normalize(s - 1)
-            if s - 4 in product:
+            if 0 <= s - 4 < DIRECT:
                 add_base(s - 4, every_site)
-            if live(s - 2):
+            if s >= 2:
                 gate(s - 2, 0)
             row_max(s, 1)
             exponentiate(s)
             if 0 <= s - 3 < DIRECT:
                 drain_product(s - 3)
-            if live(s + 1):
+            if s < LAST:
                 emissions(s + 1)
-            if live(s - 2):
+            if s >= 2:
                 gate(s - 2, 1)
             if s == 0:
-                constants()
+                make_divisor()
             if s == 2:
-                shifts()
-            for piece in pending:
-                if on_vector(piece):
-                    stage(piece, on_vector=True)
-            fillers = [partial(quantize, piece) for piece in sorted(pending, key=on_vector)]
+                make_shift()
+
+            fillers = [partial(quantize, piece) for piece in pending]
             if s - 3 >= DIRECT:
                 fillers.insert(0, partial(add_base, s - 3, every_site))
             for job in fillers[:1]:
                 job()
-            if live(s - 2):
+            if s >= 2:
                 quantize_z(s - 2, 1)
             for job in fillers[1:-1]:
                 job()
@@ -360,48 +348,48 @@ def tile_listephenswindowforwardimputation_x1_kernel(tc, obs, typed, rho, g, alt
                 job()
             if s >= LAG:
                 invert(s)
-            if s == 0:
-                for piece in pieces(-1):
-                    turn(piece, "o")
-            if live(s - 1):
-                turn_posterior(s - 1, "z")
-            for piece in now:
-                turn(piece, "in")
-            if live(s - 2):
-                impute(s - 2, every_site, "o")
-            pending = (pieces(-1) if s == 0 else []) + now
-            carried = [piece for piece in now if piece[0] == "rows"]
-            for piece in pending:
-                if piece not in carried and not on_vector(piece):
-                    stage(piece, on_vector=False)
 
-        last = TILES - 1
-        normalize(last)
-        turn_posterior(last, "in")
-        for grp in range(GROUPS):
-            gate(last - 1, grp)
-        add_base(last - 2, every_site)
-        quantize_z(last - 1, 1)
-        impute(last - 1, every_site, "o")
-        for grp in range(GROUPS):
-            gate(last, grp)
-        quantize_z(last, GROUPS)
-        add_base(last - 1, every_site)
-        quarters = [slice(n * P, (n + 1) * P) for n in range(4)]
+            early = schedule[-1] if s == 0 else []
+            for piece in early:
+                turn(piece, "o")
+            if s >= 1:
+                turn_posterior(s - 1, "z")
+            for piece in schedule[s]:
+                turn(piece, "in")
+            if s >= 2:
+                impute(s - 2, every_site, "o")
+
+            pending = early + schedule[s]
+            carried = [piece for piece in schedule[s] if piece[0] == "rows"]
+            for piece in pending:
+                if piece not in carried:
+                    lay_out(piece, nc.scalar.copy)
+
+        normalize(LAST)
+        turn_posterior(LAST, "in")
+        for a in range(PASSES):
+            gate(LAST - 1, a)
+        add_base(LAST - 2, every_site)
+        quantize_z(LAST - 1, 1)
+        impute(LAST - 1, every_site, "o")
+        for a in range(PASSES):
+            gate(LAST, a)
+        quantize_z(LAST, PASSES)
+        add_base(LAST - 1, every_site)
+        quarters = [slice(n * P, (n + 1) * P) for n in range(U // P)]
         for sites, tag in zip(quarters, ["e", "e", "z", "z"]):
-            impute(last, sites, tag)
+            impute(LAST, sites, tag)
         for sites in quarters:
-            add_base(last, sites)
-        final = work.tile([P, PACK * U], BF16, name="final", tag="final", bufs=1, align_bytes=64)
+            add_base(LAST, sites)
         w = W - 1
-        for n in range(4):
-            copy = nc.scalar.copy if n < 2 else nc.vector.tensor_copy
-            copy(out=final[:, n * BANK:(n + 1) * BANK].rearrange("p (c i t) -> p c t i", i=4, t=PACK),
-                 in_=out32[w][:, :, quarters[n]].rearrange("p t (c i) -> p c t i", i=4))
+        out_bf = work.tile([P, PACK * U], BF16, name="out_bf", tag="out_bf", bufs=1, align_bytes=64)
+        for n, sites in enumerate(quarters):
+            interleave(nc.scalar.copy if n < 2 else nc.vector.tensor_copy,
+                       out_bf[:, PACK * sites.start:PACK * sites.stop], out32[w][:, :, sites])
         for n in (0, 2, 3, 1):
             cols = slice(w * U + n * P, w * U + (n + 1) * P)
-            nc.vector.quantize_mx(out=out_codes[:, cols].bitcast(FP8X4), scales=out_scales[:, cols], in_=final[:, n * BANK:(n + 1) * BANK])
+            nc.vector.quantize_mx(out=out_codes[:, cols].bitcast(FP8X4), scales=out_scales[:, cols],
+                                  in_=out_bf[:, n * PACK * P:(n + 1) * PACK * P])
             if n % 2 == 1:
-                cols = slice(w * U + (n - 1) * P, w * U + (n + 1) * P)
-                nc.sync.dma_start(out=words_hbm[:, cols], in_=out_codes[:, cols].bitcast(I32))
+                store_words(slice(cols.stop - HALF, cols.stop))
         store_scales(range(w, W), [nc.sync, nc.scalar])

@@ -29,12 +29,11 @@ TINY = 2.0 ** -30
 
 GPSIMD_COLS = 512
 DIRECT = 11
-LAG = 3
 MAX_PIECES, MAX_LONG = 3, 2
 
 
 def piece_schedule():
-    schedule = {step: [] for step in range(-1, TILES)}
+    schedule = {step: [] for step in range(-1, TILES + 1)}
     for w in range(W):
         for n in range(2 * PASSES):
             if PACK * w - 2 + n >= 0:
@@ -45,7 +44,7 @@ def piece_schedule():
             rows[PACK * w - 5 + (n + 1) // 2].append(("rows", w, n // 2, n % 2))
     for w in range(W - 1):
         closing = PACK * w + PACK - 1
-        step = closing + (3 if closing >= DIRECT else 4)
+        step = closing + (4 if closing >= DIRECT else 5)
         for half in range(2):
             while len(schedule[step]) + len(rows[step]) >= MAX_PIECES or len(schedule[step]) >= MAX_LONG:
                 step = step + 1
@@ -306,58 +305,65 @@ def tile_listephenswindowforwardimputation_x1_kernel(tc, obs, typed, rho, g, alt
         every_site = slice(0, U)
         carried = [("alt", 0, 0, 0), ("alt", 0, 0, 1), late_obs]
         pending = carried
-        for s in range(TILES):
-            if s > LAG:
-                normalize(s - 1)
+        norm_step = {i + (1 if i < PACK else 2): i for i in range(LAST)}
+        for s in range(TILES + 1):
+            normed = norm_step.get(s)
+            gated = norm_step.get(s - 1)
+            recurs = s - 1 >= PACK
+            by_vector = [piece for piece in carried[:1] if gated is None and piece[0] == "rows"]
+            if normed is not None and normed >= PACK:
+                normalize(normed)
             for piece in carried:
-                lay_out(piece, nc.scalar.copy)
+                if piece not in by_vector:
+                    lay_out(piece, nc.scalar.copy)
 
-            row_max(s, 0)
-            if 0 < s <= LAG:
-                invert(s - 1)
-                normalize(s - 1)
+            if s < TILES:
+                row_max(s, 0)
+            if normed is not None and normed < PACK:
+                invert(normed)
+                normalize(normed)
+            if 0 <= s - 5 < DIRECT:
+                add_base(s - 5, every_site)
+            if gated is not None:
+                gate(gated, 0)
+            for piece in by_vector:
+                lay_out(piece, nc.vector.tensor_copy)
+            if s < TILES:
+                row_max(s, 1)
+                exponentiate(s)
             if 0 <= s - 4 < DIRECT:
-                add_base(s - 4, every_site)
-            if s >= 2:
-                gate(s - 2, 0)
-            row_max(s, 1)
-            exponentiate(s)
-            if 0 <= s - 3 < DIRECT:
-                drain_product(s - 3)
+                drain_product(s - 4)
             if s < LAST:
                 emissions(s + 1)
-            if s >= 2:
-                gate(s - 2, 1)
+            if gated is not None:
+                gate(gated, 1)
             if s == 0:
                 make_divisor()
             if s == 2:
                 make_shift()
 
-            fillers = [partial(quantize, piece) for piece in pending]
-            if s - 3 >= DIRECT:
-                fillers.insert(0, partial(add_base, s - 3, every_site))
-            for job in fillers[:1]:
+            jobs = [partial(quantize, piece) for piece in pending]
+            if s - 4 >= DIRECT:
+                jobs.insert(0, partial(add_base, s - 4, every_site))
+            if recurs:
+                jobs.insert(0, partial(recombine, s - 1))
+            jobs[0]()
+            if gated is not None:
+                quantize_z(gated, 1)
+            for job in jobs[1:]:
                 job()
-            if s >= 2:
-                quantize_z(s - 2, 1)
-            for job in fillers[1:-1]:
-                job()
-            if s >= PACK:
-                recombine(s)
-            for job in fillers[1:][-1:]:
-                job()
-            if s >= LAG:
-                invert(s)
+            if recurs:
+                invert(s - 1)
 
             early = schedule[-1] if s == 0 else []
             for piece in early:
                 turn(piece, "o")
-            if s >= 1:
-                turn_posterior(s - 1, "z")
+            if normed is not None:
+                turn_posterior(normed, "z")
             for piece in schedule[s]:
                 turn(piece, "in")
-            if s >= 2:
-                impute(s - 2, every_site, "o")
+            if gated is not None:
+                impute(gated, every_site, "o")
 
             pending = early + schedule[s]
             carried = [piece for piece in schedule[s] if piece[0] == "rows"]

from contextlib import ExitStack
from functools import partial

import concourse.mybir as mybir
from concourse.masks import make_identity

W, Q, H, T, U = 4, 512, 1024, 512, 512
FLOPS = 2 * W * Q * H * T + 2 * W * Q * H * U

F32 = mybir.dt.float32
BF16 = mybir.dt.bfloat16
I32 = mybir.dt.int32
U32 = mybir.dt.uint32
U8 = mybir.dt.uint8
FP8X4 = mybir.dt.float8_e4m3fn_x4
ALU = mybir.AluOpType
ACT = mybir.ActivationFunctionType

P = 128
PACK = 4
BANK = 512
PASSES = H // BANK
OBS = PASSES
HALF = 256
RUN = 4
TILES = W * PACK
LAST = TILES - 1
TINY = 2.0 ** -30

GPSIMD_COLS = 512
DIRECT = 11
MAX_PIECES, MAX_LONG = 3, 2


def piece_schedule():
    schedule = {step: [] for step in range(-1, TILES + 1)}
    for w in range(W):
        for n in range(2 * PASSES):
            if PACK * w - 2 + n >= 0:
                schedule[PACK * w - 2 + n].append(("alt", w, n // 2, n % 2))
    rows = {step: [] for step in schedule}
    for w in range(1, W):
        for n in range(2 * (PASSES + 1)):
            rows[PACK * w - 5 + (n + 1) // 2].append(("rows", w, n // 2, n % 2))
    for w in range(W - 1):
        closing = PACK * w + PACK - 1
        step = closing + (4 if closing >= DIRECT else 5)
        for half in range(2):
            while len(schedule[step]) + len(rows[step]) >= MAX_PIECES or len(schedule[step]) >= MAX_LONG:
                step = step + 1
            schedule[step].append(("out", w, 0, half))
    return {step: schedule[step] + rows[step] for step in schedule}


def tile_listephenswindowforwardimputation_x1_kernel(tc, obs, typed, rho, g, alt, base, out_0, out_1, out_2):
    nc = tc.nc
    with ExitStack() as ctx:
        keep = ctx.enter_context(tc.tile_pool(name="keep", bufs=1))
        work = ctx.enter_context(tc.tile_pool(name="work", bufs=2))
        psum = ctx.enter_context(tc.psum_pool(name="psum", bufs=2))
        ctx.enter_context(tc.manual_schedule())

        ident = keep.tile([P, P], F32, name="ident")
        make_identity(nc, ident[:])

        rows_raw = {}
        alt_raw = {}

        def load_rows(w, part, half):
            src = obs[w] if part == OBS else typed[w, part * BANK:(part + 1) * BANK, :]
            raw = keep.tile([P, 2, T], BF16, name="rows_%d_%d_%d" % (w, part, half))
            nc.sync.dma_start(out=raw[:], in_=src.rearrange("(m t) k -> m t k", t=PACK)[:, 2 * half:2 * half + 2, :])
            rows_raw[(w, part, half)] = raw

        def load_alt(w, a):
            raw = keep.tile([P, PACK, U], BF16, name="alt_%d_%d" % (w, a))
            nc.sync.dma_start(out=raw[:], in_=alt[w, a * BANK:(a + 1) * BANK, :].rearrange("(p t) u -> p t u", t=PACK))
            alt_raw[(w, a)] = raw

        g_raw = keep.tile([P, PASSES, PACK], BF16, name="g_raw")
        rho_raw = keep.tile([P, W - 1], BF16, name="rho_raw")
        base_rows = keep.tile([P, W, U], BF16, name="base_rows")
        head = [("rows", 0, OBS, 0), ("rows", 0, 0, 0), ("rows", 0, 0, 1), ("rows", 0, 1, 0), ("rows", 0, 1, 1)]
        late_obs = ("rows", 0, OBS, 1)
        for piece in head + [late_obs]:
            load_rows(*piece[1:])
        load_alt(0, 0)
        load_rows(1, 0, 0)
        load_alt(0, 1)
        nc.sync.dma_start(out=g_raw[:], in_=g.rearrange("(a p t) -> p a t", a=PASSES, t=PACK))
        nc.sync.dma_start(out=rho_raw[:], in_=rho.partition_broadcast(P))
        for w in range(1, W):
            for n in range(2 * (PASSES + 1)):
                if (w, n // 2, n % 2) not in rows_raw:
                    load_rows(w, n // 2, n % 2)
            for a in range(PASSES):
                load_alt(w, a)
            if w == 1:
                nc.sync.dma_start(out=base_rows[:].rearrange("p w u -> p (w u)"),
                                  in_=base.rearrange("w u -> (w u)").partition_broadcast(P))

        out_codes = keep.tile([P, W * U], U32, name="out_codes", align_bytes=64)
        out_scales = keep.tile([P, W * U], U8, name="out_scales", align_bytes=64)
        words_hbm = out_1[0].rearrange("p m t -> p (m t)").bitcast(I32)
        scales_hbm = out_2[0].bitcast(I32)

        def store_words(cols):
            nc.sync.dma_start(out=words_hbm[:, cols], in_=out_codes[:, cols].bitcast(I32))

        def store_scales(windows, queues):
            cols = slice(windows.start * U // 4, windows.stop * U // 4)
            for n in range(4):
                queues[n % len(queues)].dma_start(out=scales_hbm[4 * n:4 * n + 4, cols],
                                                  in_=out_scales[32 * n:32 * n + 4, :].bitcast(I32)[:, cols])

        g_scaled = keep.tile([P, PASSES, PACK], F32, name="g_scaled")
        shift = keep.tile([P, W - 1], F32, name="shift")
        divisor = keep.tile([P, W - 1], F32, name="divisor")
        inv_divisor = keep.tile([P, W - 1], F32, name="inv_divisor")

        def make_divisor():
            nc.gpsimd.tensor_scalar(out=g_scaled[:], in0=g_raw[:], scalar1=float(H), scalar2=0.0, op0=ALU.mult, op1=ALU.add)
            stay = keep.tile([P, W - 1], F32, name="stay")
            nc.gpsimd.tensor_scalar(out=stay[:], in0=rho_raw[:], scalar1=-float(H), scalar2=float(H), op0=ALU.mult, op1=ALU.add)
            guard = keep.tile([P, W - 1], F32, name="guard")
            nc.gpsimd.tensor_scalar(out=guard[:], in0=stay[:], scalar1=0.0, scalar2=TINY, op0=ALU.is_equal, op1=ALU.mult)
            nc.gpsimd.tensor_tensor(out=divisor[:], in0=stay[:], in1=guard[:], op=ALU.add)

        def make_shift():
            nc.vector.reciprocal(out=inv_divisor[:], in_=divisor[:])
            nc.gpsimd.tensor_tensor(out=shift[:], in0=rho_raw[:], in1=inv_divisor[:], op=ALU.mult)

        codes = {}
        scales = {}
        turned = {}
        staged = {}
        out32 = {}

        def turn(piece, tag):
            kind, w, part, half = piece
            if kind != "rows":
                return
            bank = psum.tile([P, PACK, P], F32, name="turned", tag=tag)
            words = rows_raw[(w, part, half)][:].bitcast(F32)
            for s in range(2):
                for u in range(2):
                    nc.tensor.transpose(bank[:, 2 * s + u, :], words[:, s, u:T // 2:2], ident[:])
            turned[piece] = bank

        def interleave(copy, dst, src):
            copy(out=dst.rearrange("p (c i t) -> p c t i", i=RUN, t=PACK), in_=src.rearrange("p t (c i) -> p c t i", i=RUN))

        def lay_out(piece, copy):
            kind, w, part, half = piece
            laid = work.tile([P, PACK * HALF], BF16, name="staged", tag="staged", bufs=6, align_bytes=64)
            if kind == "rows":
                copy(out=laid[:].bitcast(F32).rearrange("p (s m u) -> p s m u", s=2, u=2),
                     in_=turned[piece][:].rearrange("p (s u) m -> p s m u", u=2))
            else:
                src = alt_raw[(w, part)] if kind == "alt" else out32[w]
                interleave(copy, laid[:], src[:, :, half * HALF:(half + 1) * HALF])
            staged[piece] = laid

        def quantize(piece):
            kind, w, part, half = piece
            if kind == "out":
                cols = slice(w * U + half * HALF, w * U + (half + 1) * HALF)
                nc.vector.quantize_mx(out=out_codes[:, cols].bitcast(FP8X4), scales=out_scales[:, cols], in_=staged[piece][:])
                store_words(cols)
                if (w, half) == (W - 2, 1):
                    store_scales(range(0, W - 1), [nc.sync])
                return
            key = (kind, w, part)
            if key not in codes:
                tag, bufs = ("alt", 2 * PASSES) if kind == "alt" else (("obs", 2) if part == OBS else ("typed", 2 * PASSES))
                codes[key] = work.tile([P, BANK], U32, name="c_" + tag, tag="c_" + tag, bufs=bufs, align_bytes=64)
                scales[key] = work.tile([P, BANK], U8, name="s_" + tag, tag="s_" + tag, bufs=bufs, align_bytes=64)
            cols = slice(half * HALF, (half + 1) * HALF)
            nc.vector.quantize_mx(out=codes[key][:, cols].bitcast(FP8X4), scales=scales[key][:, cols], in_=staged[piece][:])

        e_bank = {}
        neg_e = {}
        neg_max = {}
        weight = {}
        total = {}
        inv_total = {}
        post = {}
        post_turned = {}
        z_bf = {}
        z_codes = {}
        z_scales = {}
        o_bank = {}
        product = {}

        def emissions(i):
            w, t = divmod(i, PACK)
            cols = slice(t * P, (t + 1) * P)
            for a in range(PASSES):
                bank = psum.tile([P, BANK], F32, name="e_bank", tag="e")
                nc.tensor.matmul_mx(out=bank[:], lhsT=codes[("rows", w, OBS)][:, cols].bitcast(FP8X4),
                                    lhsT_scale=scales[("rows", w, OBS)][:, cols],
                                    rhs=codes[("rows", w, a)][:].bitcast(FP8X4), rhs_scale=scales[("rows", w, a)][:],
                                    start=True, stop=True)
                e_bank[(i, a)] = bank

        def row_max(i, a):
            if a == 0:
                neg_e[i] = work.tile([P, H], F32, name="neg_e", tag="neg_e")
            least = work.tile([P, 1], F32, name="neg_max", tag="neg_max", bufs=4)
            nc.vector.tensor_scalar(out=neg_e[i][:, a * BANK:(a + 1) * BANK], in0=e_bank[(i, a)][:], scalar1=-1.0,
                                    scalar2=neg_max[i][:] if a else None, op0=ALU.mult, op1=ALU.min, accum_out=least[:])
            neg_max[i] = least

        def exponentiate(i):
            weight[i] = work.tile([P, H], F32, name="x", tag="x")
            if i < PACK:
                total[i] = work.tile([P, 1], F32, name="total", tag="total")
                nc.scalar.activation(out=weight[i][:], in_=neg_e[i][:], func=ACT.Exp, bias=neg_max[i][:], scale=-1.0,
                                     accum_out=total[i][:])
            else:
                nc.scalar.activation(out=weight[i][:], in_=neg_e[i][:], func=ACT.Exp, bias=neg_max[i][:], scale=-1.0)

        def recombine(i):
            w = i // PACK
            b = work.tile([P, H], F32, name="b", tag="b")
            total[i] = work.tile([P, 1], F32, name="total", tag="total")
            nc.vector.scalar_tensor_tensor(out=b[:], in0=post[i - PACK][:], scalar=shift[:, w - 1:w], in1=weight[i][:],
                                           op0=ALU.add, op1=ALU.mult, accum_out=total[i][:])
            weight[i] = b

        def invert(i):
            inv_total[i] = work.tile([P, 1], F32, name="inv_total", tag="inv_total")
            nc.vector.reciprocal(out=inv_total[i][:], in_=total[i][:])

        def normalize(i):
            post[i] = work.tile([P, H], F32, name="post", tag="post", bufs=PACK + 1)
            alone = i < PACK or DIRECT + 2 < i < LAST
            split = H if alone else GPSIMD_COLS
            nc.gpsimd.tensor_scalar(out=post[i][:, :split], in0=weight[i][:, :split], scalar1=inv_total[i][:], scalar2=0.0,
                                    op0=ALU.mult, op1=ALU.add)
            if not alone:
                nc.scalar.activation(out=post[i][:, split:], in_=weight[i][:, split:], func=ACT.Copy, scale=inv_total[i][:])

        def turn_posterior(i, tag):
            for a in range(PASSES):
                bank = psum.tile([P, PACK, P], F32, name="post_turned", tag=tag)
                for t in range(PACK):
                    first = a * BANK + t * P
                    nc.tensor.transpose(bank[:, t, :], post[i][:, first:first + P], ident[:])
                post_turned[(i, a)] = bank

        def gate(i, a):
            if a == 0:
                z_bf[i] = work.tile([P, H], BF16, name="z_bf", tag="z_bf", align_bytes=64)
            nc.vector.scalar_tensor_tensor(
                out=z_bf[i][:, a * BANK:(a + 1) * BANK].rearrange("p (q t) -> p q t", t=PACK),
                in0=post_turned[(i, a)][:].rearrange("p t q -> p q t"), scalar=1.0 / H,
                in1=g_scaled[:, a, :].unsqueeze(1).to_broadcast([P, P, PACK]), op0=ALU.subtract, op1=ALU.mult)

        def quantize_z(i, parts):
            z_codes[i] = work.tile([P, PASSES * P], U32, name="z_codes", tag="z_codes", align_bytes=64)
            z_scales[i] = work.tile([P, PASSES * P], U8, name="z_scales", tag="z_scales", align_bytes=64)
            width = PASSES * P // parts
            for n in range(parts):
                cols = slice(n * width, (n + 1) * width)
                nc.vector.quantize_mx(out=z_codes[i][:, cols].bitcast(FP8X4), scales=z_scales[i][:, cols],
                                      in_=z_bf[i][:, PACK * n * width:PACK * (n + 1) * width])

        def impute(i, sites, tag):
            w = i // PACK
            bank = psum.tile([P, sites.stop - sites.start], F32, name="o_bank", tag=tag)
            for a in range(PASSES):
                cols = slice(a * P, (a + 1) * P)
                nc.tensor.matmul_mx(out=bank[:], lhsT=z_codes[i][:, cols].bitcast(FP8X4), lhsT_scale=z_scales[i][:, cols],
                                    rhs=codes[("alt", w, a)][:, sites].bitcast(FP8X4), rhs_scale=scales[("alt", w, a)][:, sites],
                                    start=(a == 0), stop=(a == PASSES - 1))
            o_bank[(i, sites.start)] = bank

        def drain_product(i):
            product[i] = work.tile([P, U], F32, name="product", tag="product")
            nc.scalar.copy(out=product[i][:], in_=o_bank[(i, 0)][:])

        def add_base(i, sites):
            w, t = divmod(i, PACK)
            if w not in out32:
                out32[w] = work.tile([P, PACK, U], F32, name="out32", tag="out32")
            if i < DIRECT:
                nc.gpsimd.tensor_tensor(out=out32[w][:, t, sites], in0=product[i][:], in1=base_rows[:, w, sites], op=ALU.add)
            else:
                nc.vector.tensor_tensor(out=out32[w][:, t, sites], in0=o_bank[(i, sites.start)][:], in1=base_rows[:, w, sites],
                                        op=ALU.add)
            if sites.stop == U:
                nc.sync.dma_start(out=out_0[w].rearrange("(p t) u -> p t u", t=PACK)[:, t, :], in_=out32[w][:, t, :])

        for piece, tag in zip(head, ["in", "in", "z", "z", "o"]):
            turn(piece, tag)
        for n, piece in enumerate(head):
            lay_out(piece, nc.vector.tensor_copy if n == 1 else nc.scalar.copy)
        for piece in head:
            quantize(piece)
        emissions(0)
        turn(late_obs, "o")

        schedule = piece_schedule()
        every_site = slice(0, U)
        carried = [("alt", 0, 0, 0), ("alt", 0, 0, 1), late_obs]
        pending = carried
        norm_step = {i + (1 if i < PACK else 2): i for i in range(LAST)}
        for s in range(TILES + 1):
            normed = norm_step.get(s)
            gated = norm_step.get(s - 1)
            recurs = s - 1 >= PACK
            by_vector = [piece for piece in carried[:1] if gated is None and piece[0] == "rows"]
            if normed is not None and normed >= PACK:
                normalize(normed)
            for piece in carried:
                if piece not in by_vector:
                    lay_out(piece, nc.scalar.copy)

            if s < TILES:
                row_max(s, 0)
            if normed is not None and normed < PACK:
                invert(normed)
                normalize(normed)
            if 0 <= s - 5 < DIRECT:
                add_base(s - 5, every_site)
            if gated is not None:
                gate(gated, 0)
            for piece in by_vector:
                lay_out(piece, nc.vector.tensor_copy)
            if s < TILES:
                row_max(s, 1)
                exponentiate(s)
            if 0 <= s - 4 < DIRECT:
                drain_product(s - 4)
            if s < LAST:
                emissions(s + 1)
            if gated is not None:
                gate(gated, 1)
            if s == 0:
                make_divisor()
            if s == 2:
                make_shift()

            jobs = [partial(quantize, piece) for piece in pending]
            if s - 4 >= DIRECT:
                jobs.insert(0, partial(add_base, s - 4, every_site))
            if recurs:
                jobs.insert(0, partial(recombine, s - 1))
            jobs[0]()
            if gated is not None:
                quantize_z(gated, 1)
            for job in jobs[1:]:
                job()
            if recurs:
                invert(s - 1)

            early = schedule[-1] if s == 0 else []
            for piece in early:
                turn(piece, "o")
            if normed is not None:
                turn_posterior(normed, "z")
            for piece in schedule[s]:
                turn(piece, "in")
            if gated is not None:
                impute(gated, every_site, "o")

            pending = early + schedule[s]
            carried = [piece for piece in schedule[s] if piece[0] == "rows"]
            for piece in pending:
                if piece not in carried:
                    lay_out(piece, nc.scalar.copy)

        normalize(LAST)
        turn_posterior(LAST, "in")
        for a in range(PASSES):
            gate(LAST - 1, a)
        add_base(LAST - 2, every_site)
        quantize_z(LAST - 1, 1)
        impute(LAST - 1, every_site, "o")
        for a in range(PASSES):
            gate(LAST, a)
        quantize_z(LAST, PASSES)
        add_base(LAST - 1, every_site)
        quarters = [slice(n * P, (n + 1) * P) for n in range(U // P)]
        for sites, tag in zip(quarters, ["e", "e", "z", "z"]):
            impute(LAST, sites, tag)
        for sites in quarters:
            add_base(LAST, sites)
        w = W - 1
        out_bf = work.tile([P, PACK * U], BF16, name="out_bf", tag="out_bf", bufs=1, align_bytes=64)
        for n, sites in enumerate(quarters):
            interleave(nc.scalar.copy if n < 2 else nc.vector.tensor_copy,
                       out_bf[:, PACK * sites.start:PACK * sites.stop], out32[w][:, :, sites])
        for n in (0, 2, 3, 1):
            cols = slice(w * U + n * P, w * U + (n + 1) * P)
            nc.vector.quantize_mx(out=out_codes[:, cols].bitcast(FP8X4), scales=out_scales[:, cols],
                                  in_=out_bf[:, n * PACK * P:(n + 1) * PACK * P])
            if n % 2 == 1:
                store_words(slice(cols.stop - HALF, cols.stop))
        store_scales(range(w, W), [nc.sync, nc.scalar])
